import numpy as np
import ml_dtypes


def mxq(x, axis, fmt="e4m3"):
    dtype, down = {"e4m3": (ml_dtypes.float8_e4m3fn, 7), "e5m2": (ml_dtypes.float8_e5m2, 14)}[fmt]
    v = np.moveaxis(np.asarray(x, np.float32).astype(ml_dtypes.bfloat16).astype(np.float64), axis, -1)
    blocks = v.reshape(v.shape[:-1] + (-1, 32))
    amax = np.abs(blocks).max(-1, keepdims=True)
    byte = np.maximum(np.where(amax > 0, np.frexp(amax)[1] - 1 + 127, 0) - down, 1)
    scale = np.exp2(byte - 127.0)
    codes = (blocks / scale).astype(np.float32).astype(dtype).astype(np.float64)
    return np.moveaxis((codes * scale).reshape(v.shape), -1, axis)


WIDE = False


def mx_kscale(k):
    if not WIDE:
        return np.ones(k)
    levels = np.array([10, -10, 5, -5, 0])
    if k % 512:
        return np.exp2(np.random.permutation(np.resize(levels, k // 32))).repeat(32)
    a = np.empty((k // 512, 16))
    for p in range(k // 512):
        a[p, :8] = np.random.permutation(np.resize(levels, 8))
        for g in range(8):
            far = levels[np.abs(levels - a[p, g]) >= 10]
            a[p, g + 8] = far[np.random.randint(len(far))]
    return np.exp2(a.ravel()).repeat(32)


def f64(x):
    return np.asarray(x).astype(np.float64)


def striped(idx):
    return np.tile(np.asarray(idx).reshape(-1, 16).T, (8, 1)).astype(np.uint16)


def unstriped(offs):
    return offs[:16].T.reshape(-1).astype(np.int64)


E2M1 = np.array([0.0, 0.5, 1.0, 1.5, 2.0, 3.0, 4.0, 6.0, -0.0, -0.5, -1.0, -1.5, -2.0, -3.0, -4.0, -6.0])


def pack_weight(w, fmt):
    k, n = w.shape
    w = f64(np.asarray(w, np.float32).astype(ml_dtypes.bfloat16)).reshape(k // 32, 32, n)
    amax = np.abs(w).max(1)
    if fmt == "e4m3":
        byte = np.frexp(amax)[1] - 1 + 127 - 7
    else:
        mant, ex = np.frexp(amax / 6.0)
        byte = np.where(mant > 0.5, ex, ex - 1) + 127
    byte = np.clip(np.where(amax > 0, byte, 1), 1, 254)
    scaled = (w * np.exp2(127.0 - byte)[:, None, :]).reshape(k, n).astype(np.float32)
    by_word = np.ascontiguousarray(scaled.reshape(k // 512, 128, 4, n).transpose(0, 1, 3, 2))
    if fmt == "e4m3":
        words = by_word.astype(ml_dtypes.float8_e4m3fn).view(np.uint8)
    else:
        c = by_word.astype(ml_dtypes.float4_e2m1fn).view(np.uint8) & 0xF
        words = (c[..., 0::2] | (c[..., 1::2] << 4)).reshape(k // 512, 128, 2 * n)
    return np.ascontiguousarray(words), np.ascontiguousarray(byte.astype(np.uint8).reshape(k // 512, 16, n))


def unpack_weight(words, scales, fmt):
    g, _, n = scales.shape
    words = np.ascontiguousarray(words).reshape(g, 128, n, -1)
    if fmt == "e4m3":
        vals = words.view(ml_dtypes.float8_e4m3fn).astype(np.float64)
    else:
        nib = np.empty((g, 128, n, 4), np.uint8)
        nib[..., 0::2] = words & 0xF
        nib[..., 1::2] = words >> 4
        vals = E2M1[nib]
    vals = vals * np.repeat(np.exp2(scales.astype(np.float64) - 127.0), 8, axis=1)[..., None]
    return vals.transpose(0, 1, 3, 2).reshape(g * 512, n)


def softplus(v):
    return np.log(1.0 + np.exp(v))


def sigmoid(v):
    return 1.0 / (1.0 + np.exp(-v))


D, E, T, I, Q, G = 512, 512, 2048, 512, 128, 32


def setup_inputs():
    n = np.random.standard_normal
    idx = np.random.permutation(T)[:I]
    fd = mx_kscale(D)
    fe = mx_kscale(E)
    keysp = pack_weight(n((D, T)) / fd[:, None], "e2m1")
    valsp = pack_weight(n((E, T)) / fe[:, None], "e2m1")
    return {
        "query": (n((D, Q)) * 1.0 / np.sqrt(D) * fd[:, None]).astype(np.float32),
        "keys_words": keysp[0],
        "keys_scales": keysp[1],
        "margin": (np.random.uniform(-0.5, 0.5, (Q, 1))).astype(np.float32),
        "reserve": (np.random.uniform(5.0, 20.0, (Q, 1))).astype(np.float32),
        "gout": (n((E, Q)) * 1 / np.sqrt(E) * fe[:, None]).astype(np.float32),
        "vals_words": valsp[0],
        "vals_scales": valsp[1],
        "old": (0.5 * n((Q, T))).astype(np.float32),
        "offs": striped(idx),
    }


def reference(query, keys_words, keys_scales, margin, reserve, gout, vals_words, vals_scales, old, offs):
    idx = unstriped(offs)
    keysu = unpack_weight(keys_words, keys_scales, "e2m1")
    valsu = unpack_weight(vals_words, vals_scales, "e2m1")
    queryq = mxq(f64(query), 0, "e4m3")
    keysidxg = keysu[:, idx]
    a = queryq.T @ keysidxg
    m1 = a.reshape(Q, G, I // G).mean(axis=2)
    mr = np.repeat(m1, I // G, axis=1)
    p = softplus(a - mr - f64(margin))
    n2 = np.sqrt(np.sum(np.square(p), axis=1, keepdims=True) + f64(reserve))
    goutq = mxq(f64(gout), 0, "e4m3")
    valsidxg = valsu[:, idx]
    c0 = goutq.T @ valsidxg
    dn2 = np.sum(c0 * p / np.square(n2) * (-1.0), axis=1, keepdims=True)
    dp = c0 / n2 + dn2 * 0.5 / np.sqrt(np.sum(np.square(p), axis=1, keepdims=True) + f64(reserve)) * p * 2.0
    dmr = dp * sigmoid(a - mr - f64(margin)) * (-1.0)
    dm1 = dmr.reshape(Q, G, I // G).sum(axis=2)
    e1 = dm1 / 16.0
    r1 = np.repeat(e1, I // G, axis=1)
    da = dp * sigmoid(a - mr - f64(margin)) + r1
    gs = da * 16.0
    gf = np.zeros((Q, T))
    gf[:, idx] = gs
    y = f64(old) + gf
    return y

@@ -1,0 +1,215 @@
+from contextlib import ExitStack
+
+import concourse.mybir as mybir
+
+D, E, T, SLOTS, Q, PAGES = 512, 512, 2048, 512, 128, 32
+PAGE = SLOTS // PAGES
+FLOPS = 2 * Q * SLOTS * (D + E)
+
+F32 = mybir.dt.float32
+BF16 = mybir.dt.bfloat16
+I32 = mybir.dt.int32
+U32 = mybir.dt.uint32
+U16 = mybir.dt.uint16
+U8 = mybir.dt.uint8
+FP8X4 = mybir.dt.float8_e4m3fn_x4
+FP4X4 = mybir.dt.float4_e2m1fn_x4
+ALU = mybir.AluOpType
+ACT = mybir.ActivationFunctionType
+AXIS_X = mybir.AxisListType.X
+
+P = 128
+PACK = 4
+HALF = SLOTS // 2
+HALF_PAGES = PAGES // 2
+LIST_COLS = SLOTS // 16
+LN_FLOOR = 2.0 ** -60
+STORE_WIDTHS = (256, 512, 512, 512, 256)
+
+
+def load_scale_rows(nc, tile, scales):
+    for quad in range(4):
+        nc.sync.dma_start(
+            out=tile[32 * quad : 32 * quad + 4, :].bitcast(I32),
+            in_=scales[0, 4 * quad : 4 * quad + 4, :].bitcast(I32),
+        )
+
+
+def by_page(ap):
+    return ap.rearrange("p (g j) -> p g j", j=PAGE)
+
+
+def over_page(ap):
+    return ap.unsqueeze(2).to_broadcast([P, ap.shape[1], PAGE])
+
+
+def tile_attend_bsharedthreshold_s_kernel(
+    tc, query, keys_words, keys_scales, margin, reserve, gout, vals_words, vals_scales, old, offs, out
+):
+    nc = tc.nc
+    with ExitStack() as ctx:
+        sb = ctx.enter_context(tc.tile_pool(name="sb", bufs=1))
+        psum = ctx.enter_context(tc.psum_pool(name="psum", bufs=1))
+
+        offsets = sb.tile([P, LIST_COLS], U16, name="offsets")
+        key_pool = sb.tile([P, T], U16, name="key_pool", tag="key_buf", align_bytes=64)
+        key_scale_pool = sb.tile([P, T], U8, name="key_scale_pool")
+        val_pool = sb.tile([P, T], U16, name="val_pool", tag="val_buf", align_bytes=64)
+        val_scale_pool = sb.tile([P, T], U8, name="val_scale_pool")
+        q_raw = sb.tile([P, PACK, Q], F32, name="q_raw")
+        g_raw = sb.tile([P, PACK, Q], F32, name="g_raw")
+        margin_col = sb.tile([P, 1], F32, name="margin_col")
+        reserve_col = sb.tile([P, 1], F32, name="reserve_col")
+        total = sb.tile([P, T], F32, name="total")
+        placed = sb.tile([P, T], F32, name="placed")
+        zero_col = sb.tile([P, 1], F32, name="zero_col")
+
+        nc.gpsimd.memset(zero_col[:], 0.0)
+        nc.vector.memset(key_scale_pool[:].bitcast(I32), 0)
+        nc.vector.memset(val_scale_pool[:].bitcast(I32), 0)
+        nc.vector.memset(placed[:], 0.0)
+
+        nc.sync.dma_start(offsets[:], offs)
+        nc.sync.dma_start(out=key_pool[:].bitcast(I32), in_=keys_words[0].bitcast(I32))
+        nc.sync.dma_start(out=q_raw[:], in_=query.rearrange("(p j) q -> p j q", j=PACK))
+        nc.sync.dma_start(out=margin_col[:], in_=margin)
+        load_scale_rows(nc, key_scale_pool, keys_scales)
+        nc.sync.dma_start(out=g_raw[:], in_=gout.rearrange("(p j) q -> p j q", j=PACK))
+        nc.sync.dma_start(out=val_pool[:].bitcast(I32), in_=vals_words[0].bitcast(I32))
+        load_scale_rows(nc, val_scale_pool, vals_scales)
+        nc.sync.dma_start(out=reserve_col[:], in_=reserve)
+        nc.sync.dma_start(out=total[:], in_=old)
+
+        half_col = sb.tile([P, 1], F32, name="half_col")
+        nc.scalar.activation(half_col[:], zero_col[:], ACT.Sigmoid)
+        minus_half = sb.tile([P, 1], F32, name="minus_half")
+        nc.gpsimd.tensor_scalar(minus_half[:], half_col[:], -1.0, 0.0, ALU.mult, ALU.add)
+
+        q_grouped = sb.tile([P, Q, PACK], BF16, name="q_grouped", align_bytes=64)
+        g_grouped = sb.tile([P, Q, PACK], BF16, name="g_grouped", align_bytes=64)
+        nc.scalar.copy(q_grouped[:], q_raw[:].rearrange("p j q -> p q j"))
+        nc.scalar.copy(g_grouped[:], g_raw[:].rearrange("p j q -> p q j"))
+
+        key_words = sb.tile([P, SLOTS], U16, name="key_words", align_bytes=64)
+        nc.vector.tensor_copy(key_words[:], key_pool[:].indirect(offsets[:]))
+        q_codes = sb.tile([P, Q], U32, name="q_codes", align_bytes=64)
+        q_scales = sb.tile([P, Q], U8, name="q_scales", align_bytes=64)
+        nc.vector.quantize_mx(
+            out=q_codes[:].bitcast(FP8X4), scales=q_scales[:], in_=q_grouped[:].rearrange("p q j -> p (q j)")
+        )
+        key_bytes = sb.tile([P, SLOTS], U8, name="key_bytes", tag="key_buf", align_bytes=64)
+        halves = [slice(h * HALF, (h + 1) * HALF) for h in range(2)]
+        page_halves = [slice(h * HALF_PAGES, (h + 1) * HALF_PAGES) for h in range(2)]
+        list_halves = [offsets[:, h * LIST_COLS // 2 : (h + 1) * LIST_COLS // 2] for h in range(2)]
+        scores = [psum.tile([P, HALF], F32, name="scores%d" % h) for h in range(2)]
+        for h in range(2):
+            nc.vector.tensor_copy(key_bytes[:, halves[h]], key_scale_pool[:].indirect(list_halves[h]))
+            nc.tensor.matmul_mx(
+                out=scores[h][:],
+                lhsT=q_codes[:].bitcast(FP8X4),
+                lhsT_scale=q_scales[:],
+                rhs=key_words[:, halves[h]].bitcast(FP4X4),
+                rhs_scale=key_bytes[:, halves[h]],
+                start=True,
+                stop=True,
+            )
+
+        g_codes = sb.tile([P, Q], U32, name="g_codes", align_bytes=64)
+        g_scales = sb.tile([P, Q], U8, name="g_scales", align_bytes=64)
+
+        page_sums = sb.tile([P, PAGES], F32, name="page_sums", tag="sum_buf", align_bytes=64)
+        below = sb.tile([P, SLOTS], F32, name="below")
+        sig_neg = sb.tile([P, SLOTS], F32, name="sig_neg")
+        for h in range(2):
+            nc.vector.tensor_reduce(page_sums[:, page_halves[h]], by_page(scores[h][:]), AXIS_X, ALU.add)
+        for h in range(2):
+            nc.vector.scalar_tensor_tensor(
+                by_page(below[:, halves[h]]),
+                over_page(page_sums[:, page_halves[h]]),
+                1.0 / PAGE,
+                by_page(scores[h][:]),
+                ALU.mult,
+                ALU.subtract,
+            )
+            nc.scalar.activation(sig_neg[:, halves[h]], below[:, halves[h]], ACT.Sigmoid, bias=margin_col[:])
+
+        val_words = sb.tile([P, SLOTS], U16, name="val_words", tag="sum_buf", align_bytes=64)
+        nc.vector.tensor_copy(val_words[:], val_pool[:].indirect(offsets[:]))
+        nc.vector.quantize_mx(
+            out=g_codes[:].bitcast(FP8X4), scales=g_scales[:], in_=g_grouped[:].rearrange("p q j -> p (q j)")
+        )
+        val_bytes = sb.tile([P, SLOTS], U8, name="val_bytes", tag="val_buf", align_bytes=64)
+        nc.vector.tensor_copy(val_bytes[:], val_scale_pool[:].indirect(offsets[:]))
+        c0 = psum.tile([P, SLOTS], F32, name="c0")
+        nc.tensor.matmul_mx(
+            out=c0[:],
+            lhsT=g_codes[:].bitcast(FP8X4),
+            lhsT_scale=g_scales[:],
+            rhs=val_words[:].bitcast(FP4X4),
+            rhs_scale=val_bytes[:],
+            start=True,
+            stop=True,
+        )
+
+        def inner(tile):
+            return tile[:].rearrange("p (c w) -> p c w", c=4)[:, 1:3, :]
+
+        def outer(tile):
+            return tile[:].rearrange("p (c w) -> p c w", c=4)[:, 0:4:3, :]
+
+        log_sig = sb.tile([P, SLOTS], F32, name="log_sig")
+        neg_p = sb.tile([P, SLOTS], F32, name="neg_p")
+        squares = sb.tile([P, SLOTS], F32, name="squares")
+        sq_inner = sb.tile([P, 1], F32, name="sq_inner")
+        sq_outer = sb.tile([P, 1], F32, name="sq_outer", tag="late_buf")
+        for part in (inner, outer):
+            nc.scalar.activation(part(log_sig), part(sig_neg), ACT.Ln, bias=LN_FLOOR)
+        for part in (inner, outer):
+            nc.vector.scalar_tensor_tensor(
+                part(neg_p), part(below), margin_col[:], part(log_sig), ALU.add, ALU.min
+            )
+        partial = sb.tile([P, 1], F32, name="partial")
+        norm_sq = sb.tile([P, 1], F32, name="norm_sq")
+        nc.scalar.activation(inner(squares), inner(neg_p), ACT.Square, accum_out=sq_inner[:])
+        nc.scalar.activation(partial[:], sq_inner[:], ACT.Identity, bias=reserve_col[:])
+        nc.scalar.activation(outer(squares), outer(neg_p), ACT.Square, accum_out=sq_outer[:])
+        nc.scalar.activation(norm_sq[:], sq_outer[:], ACT.Identity, bias=partial[:])
+
+        products = sb.tile([P, SLOTS], F32, name="products")
+        dot = sb.tile([P, 1], F32, name="dot")
+        nc.vector.scalar_tensor_tensor(products[:], c0[:], -1.0, neg_p[:], ALU.mult, ALU.mult, accum_out=dot[:])
+        inv_norm_sq = sb.tile([P, 1], F32, name="inv_norm_sq")
+        nc.vector.reciprocal(inv_norm_sq[:], norm_sq[:])
+        inv_norm = sb.tile([P, 1], F32, name="inv_norm")
+        nc.gpsimd.tensor_tensor(inv_norm[:], norm_sq[:], minus_half[:], ALU.pow)
+        sig16 = sb.tile([P, SLOTS], F32, name="sig16", tag="late_buf")
+        nc.scalar.activation(sig16[:], sig_neg[:], ACT.Identity, bias=16.0, scale=-16.0)
+
+        pull = sb.tile([P, 1], F32, name="pull")
+        nc.vector.tensor_tensor(pull[:], dot[:], inv_norm_sq[:], ALU.mult)
+        dp_n2 = sb.tile([P, SLOTS], F32, name="dp_n2")
+        nc.vector.scalar_tensor_tensor(dp_n2[:], neg_p[:], pull[:], c0[:], ALU.mult, ALU.add)
+        direct = sb.tile([P, SLOTS], F32, name="direct")
+        direct_sums = sb.tile([P, PAGES], F32, name="direct_sums")
+        shared = sb.tile([P, SLOTS], F32, name="shared")
+        for h in range(2):
+            nc.vector.scalar_tensor_tensor(
+                direct[:, halves[h]], dp_n2[:, halves[h]], inv_norm[:], sig16[:, halves[h]], ALU.mult, ALU.mult
+            )
+        for h in range(2):
+            nc.vector.tensor_reduce(direct_sums[:, page_halves[h]], by_page(direct[:, halves[h]]), AXIS_X, ALU.add)
+            nc.scalar.activation(
+                by_page(shared[:, halves[h]]), over_page(direct_sums[:, page_halves[h]]), ACT.Copy, scale=-1.0 / PAGE
+            )
+        for h in range(2):
+            nc.vector.tensor_tensor(
+                placed[:].indirect(list_halves[h]), direct[:, halves[h]], shared[:, halves[h]], ALU.add
+            )
+
+        start = 0
+        for n, width in enumerate(STORE_WIDTHS):
+            cols = slice(start, start + width)
+            nc.vector.tensor_tensor(total[:, cols], total[:, cols], placed[:, cols], ALU.add)
+            queue = nc.sync if n % 2 == 0 else nc.scalar
+            queue.dma_start(out=out[:, cols], in_=total[:, cols])
+            start += width

@@ -24,15 +24,12 @@ HALF = SLOTS // 2
 HALF_PAGES = PAGES // 2
 LIST_COLS = SLOTS // 16
 LN_FLOOR = 2.0 ** -60
-STORE_WIDTHS = (256, 512, 512, 512, 256)
+STORE_WIDTHS = (384, 384, 384, 384, 384, 128)
 
 
 def load_scale_rows(nc, tile, scales):
-    for quad in range(4):
-        nc.sync.dma_start(
-            out=tile[32 * quad : 32 * quad + 4, :].bitcast(I32),
-            in_=scales[0, 4 * quad : 4 * quad + 4, :].bitcast(I32),
-        )
+    for row in range(4):
+        nc.sync.dma_start(out=tile[row:P:32, :].bitcast(I32), in_=scales[0, row:16:4, :].bitcast(I32))
 
 
 def by_page(ap):
@@ -52,11 +49,11 @@ def tile_attend_bsharedthreshold_s_kernel(
         psum = ctx.enter_context(tc.psum_pool(name="psum", bufs=1))
 
         offsets = sb.tile([P, LIST_COLS], U16, name="offsets")
-        key_pool = sb.tile([P, T], U16, name="key_pool", tag="key_buf", align_bytes=64)
-        key_scale_pool = sb.tile([P, T], U8, name="key_scale_pool")
-        val_pool = sb.tile([P, T], U16, name="val_pool", tag="val_buf", align_bytes=64)
+        key_pool = sb.tile([P, T], U16, name="key_pool")
+        key_scale_pool = sb.tile([P, T], U8, name="key_scale_pool", tag="key_buf", align_bytes=64)
+        val_pool = sb.tile([P, T], U16, name="val_pool")
         val_scale_pool = sb.tile([P, T], U8, name="val_scale_pool")
-        q_raw = sb.tile([P, PACK, Q], F32, name="q_raw")
+        q_raw = sb.tile([P, PACK, Q], F32, name="q_raw", tag="operand_a", align_bytes=64)
         g_raw = sb.tile([P, PACK, Q], F32, name="g_raw")
         margin_col = sb.tile([P, 1], F32, name="margin_col")
         reserve_col = sb.tile([P, 1], F32, name="reserve_col")
@@ -67,15 +64,16 @@ def tile_attend_bsharedthreshold_s_kernel(
         nc.gpsimd.memset(zero_col[:], 0.0)
         nc.vector.memset(key_scale_pool[:].bitcast(I32), 0)
         nc.vector.memset(val_scale_pool[:].bitcast(I32), 0)
-        nc.vector.memset(placed[:], 0.0)
+        nc.vector.memset(placed[:, 0 : T // 2].bitcast(I32), 0)
+        nc.gpsimd.memset(placed[:, T // 2 : T].bitcast(I32), 0)
 
-        nc.sync.dma_start(offsets[:], offs)
         nc.sync.dma_start(out=key_pool[:].bitcast(I32), in_=keys_words[0].bitcast(I32))
-        nc.sync.dma_start(out=q_raw[:], in_=query.rearrange("(p j) q -> p j q", j=PACK))
-        nc.sync.dma_start(out=margin_col[:], in_=margin)
+        nc.sync.dma_start(offsets[:], offs)
         load_scale_rows(nc, key_scale_pool, keys_scales)
+        nc.sync.dma_start(out=q_raw[:], in_=query.rearrange("(p j) q -> p j q", j=PACK))
         nc.sync.dma_start(out=g_raw[:], in_=gout.rearrange("(p j) q -> p j q", j=PACK))
         nc.sync.dma_start(out=val_pool[:].bitcast(I32), in_=vals_words[0].bitcast(I32))
+        nc.sync.dma_start(out=margin_col[:], in_=margin)
         load_scale_rows(nc, val_scale_pool, vals_scales)
         nc.sync.dma_start(out=reserve_col[:], in_=reserve)
         nc.sync.dma_start(out=total[:], in_=old)
@@ -87,37 +85,46 @@ def tile_attend_bsharedthreshold_s_kernel(
 
         q_grouped = sb.tile([P, Q, PACK], BF16, name="q_grouped", align_bytes=64)
         g_grouped = sb.tile([P, Q, PACK], BF16, name="g_grouped", align_bytes=64)
-        nc.scalar.copy(q_grouped[:], q_raw[:].rearrange("p j q -> p q j"))
-        nc.scalar.copy(g_grouped[:], g_raw[:].rearrange("p j q -> p q j"))
+        for grouped, raw in ((q_grouped, q_raw), (g_grouped, g_raw)):
+            nc.scalar.copy(
+                grouped[:].rearrange("p (c i) j -> p c j i", i=4), raw[:].rearrange("p j (c i) -> p c j i", i=4)
+            )
 
-        key_words = sb.tile([P, SLOTS], U16, name="key_words", align_bytes=64)
-        nc.vector.tensor_copy(key_words[:], key_pool[:].indirect(offsets[:]))
-        q_codes = sb.tile([P, Q], U32, name="q_codes", align_bytes=64)
-        q_scales = sb.tile([P, Q], U8, name="q_scales", align_bytes=64)
-        nc.vector.quantize_mx(
-            out=q_codes[:].bitcast(FP8X4), scales=q_scales[:], in_=q_grouped[:].rearrange("p q j -> p (q j)")
-        )
-        key_bytes = sb.tile([P, SLOTS], U8, name="key_bytes", tag="key_buf", align_bytes=64)
         halves = [slice(h * HALF, (h + 1) * HALF) for h in range(2)]
         page_halves = [slice(h * HALF_PAGES, (h + 1) * HALF_PAGES) for h in range(2)]
         list_halves = [offsets[:, h * LIST_COLS // 2 : (h + 1) * LIST_COLS // 2] for h in range(2)]
+        key_words = sb.tile([P, SLOTS], U16, name="key_words", tag="operand_b", align_bytes=64)
+        key_bytes = [
+            sb.tile([P, HALF], U8, name="key_bytes0", align_bytes=64),
+            sb.tile([P, HALF], U8, name="key_bytes1", tag="operand_a", align_bytes=64),
+        ]
+        q_codes = sb.tile([P, Q], U32, name="q_codes", align_bytes=64)
+        q_scales = sb.tile([P, Q], U8, name="q_scales", align_bytes=64)
+        nc.vector.tensor_copy(key_words[:], key_pool[:].indirect(offsets[:]))
+        nc.vector.tensor_copy(key_bytes[0][:], key_scale_pool[:].indirect(list_halves[0]))
+        nc.vector.quantize_mx(
+            out=q_codes[:].bitcast(FP8X4), scales=q_scales[:], in_=q_grouped[:].rearrange("p q j -> p (q j)")
+        )
+        nc.vector.tensor_copy(key_bytes[1][:], key_scale_pool[:].indirect(list_halves[1]))
         scores = [psum.tile([P, HALF], F32, name="scores%d" % h) for h in range(2)]
         for h in range(2):
-            nc.vector.tensor_copy(key_bytes[:, halves[h]], key_scale_pool[:].indirect(list_halves[h]))
             nc.tensor.matmul_mx(
                 out=scores[h][:],
                 lhsT=q_codes[:].bitcast(FP8X4),
                 lhsT_scale=q_scales[:],
                 rhs=key_words[:, halves[h]].bitcast(FP4X4),
-                rhs_scale=key_bytes[:, halves[h]],
+                rhs_scale=key_bytes[h][:],
                 start=True,
                 stop=True,
             )
 
-        g_codes = sb.tile([P, Q], U32, name="g_codes", align_bytes=64)
+        g_codes = sb.tile([P, Q], U32, name="g_codes", tag="key_buf", align_bytes=64)
         g_scales = sb.tile([P, Q], U8, name="g_scales", align_bytes=64)
+        nc.vector.quantize_mx(
+            out=g_codes[:].bitcast(FP8X4), scales=g_scales[:], in_=g_grouped[:].rearrange("p q j -> p (q j)")
+        )
 
-        page_sums = sb.tile([P, PAGES], F32, name="page_sums", tag="sum_buf", align_bytes=64)
+        page_sums = sb.tile([P, PAGES], F32, name="page_sums")
         below = sb.tile([P, SLOTS], F32, name="below")
         sig_neg = sb.tile([P, SLOTS], F32, name="sig_neg")
         for h in range(2):
@@ -133,23 +140,21 @@ def tile_attend_bsharedthreshold_s_kernel(
             )
             nc.scalar.activation(sig_neg[:, halves[h]], below[:, halves[h]], ACT.Sigmoid, bias=margin_col[:])
 
-        val_words = sb.tile([P, SLOTS], U16, name="val_words", tag="sum_buf", align_bytes=64)
+        val_words = sb.tile([P, SLOTS], U16, name="val_words", tag="operand_b", align_bytes=64)
         nc.vector.tensor_copy(val_words[:], val_pool[:].indirect(offsets[:]))
-        nc.vector.quantize_mx(
-            out=g_codes[:].bitcast(FP8X4), scales=g_scales[:], in_=g_grouped[:].rearrange("p q j -> p (q j)")
-        )
-        val_bytes = sb.tile([P, SLOTS], U8, name="val_bytes", tag="val_buf", align_bytes=64)
-        nc.vector.tensor_copy(val_bytes[:], val_scale_pool[:].indirect(offsets[:]))
+        val_bytes = sb.tile([P, SLOTS], U8, name="val_bytes", tag="operand_a", align_bytes=64)
         c0 = psum.tile([P, SLOTS], F32, name="c0")
-        nc.tensor.matmul_mx(
-            out=c0[:],
-            lhsT=g_codes[:].bitcast(FP8X4),
-            lhsT_scale=g_scales[:],
-            rhs=val_words[:].bitcast(FP4X4),
-            rhs_scale=val_bytes[:],
-            start=True,
-            stop=True,
-        )
+        for h in range(2):
+            nc.vector.tensor_copy(val_bytes[:, halves[h]], val_scale_pool[:].indirect(list_halves[h]))
+            nc.tensor.matmul_mx(
+                out=c0[:, halves[h]],
+                lhsT=g_codes[:].bitcast(FP8X4),
+                lhsT_scale=g_scales[:],
+                rhs=val_words[:, halves[h]].bitcast(FP4X4),
+                rhs_scale=val_bytes[:, halves[h]],
+                start=True,
+                stop=True,
+            )
 
         def inner(tile):
             return tile[:].rearrange("p (c w) -> p c w", c=4)[:, 1:3, :]
@@ -176,8 +181,12 @@ def tile_attend_bsharedthreshold_s_kernel(
         nc.scalar.activation(norm_sq[:], sq_outer[:], ACT.Identity, bias=partial[:])
 
         products = sb.tile([P, SLOTS], F32, name="products")
-        dot = sb.tile([P, 1], F32, name="dot")
-        nc.vector.scalar_tensor_tensor(products[:], c0[:], -1.0, neg_p[:], ALU.mult, ALU.mult, accum_out=dot[:])
+        dot_inner = sb.tile([P, 1], F32, name="dot_inner")
+        dot_outer = sb.tile([P, 1], F32, name="dot_outer")
+        for part, dot in ((inner, dot_inner), (outer, dot_outer)):
+            nc.vector.scalar_tensor_tensor(
+                part(products), part(c0), -1.0, part(neg_p), ALU.mult, ALU.mult, accum_out=dot[:]
+            )
         inv_norm_sq = sb.tile([P, 1], F32, name="inv_norm_sq")
         nc.vector.reciprocal(inv_norm_sq[:], norm_sq[:])
         inv_norm = sb.tile([P, 1], F32, name="inv_norm")
@@ -186,9 +195,12 @@ def tile_attend_bsharedthreshold_s_kernel(
         nc.scalar.activation(sig16[:], sig_neg[:], ACT.Identity, bias=16.0, scale=-16.0)
 
         pull = sb.tile([P, 1], F32, name="pull")
-        nc.vector.tensor_tensor(pull[:], dot[:], inv_norm_sq[:], ALU.mult)
+        nc.vector.tensor_scalar(pull[:], dot_inner[:], dot_outer[:], inv_norm_sq[:], ALU.add, ALU.mult)
         dp_n2 = sb.tile([P, SLOTS], F32, name="dp_n2")
-        nc.vector.scalar_tensor_tensor(dp_n2[:], neg_p[:], pull[:], c0[:], ALU.mult, ALU.add)
+        for h in range(2):
+            nc.vector.scalar_tensor_tensor(
+                dp_n2[:, halves[h]], neg_p[:, halves[h]], pull[:], c0[:, halves[h]], ALU.mult, ALU.add
+            )
         direct = sb.tile([P, SLOTS], F32, name="direct")
         direct_sums = sb.tile([P, PAGES], F32, name="direct_sums")
         shared = sb.tile([P, SLOTS], F32, name="shared")

from contextlib import ExitStack

import concourse.mybir as mybir

D, E, T, SLOTS, Q, PAGES = 512, 512, 2048, 512, 128, 32
PAGE = SLOTS // PAGES
FLOPS = 2 * Q * SLOTS * (D + E)

F32 = mybir.dt.float32
BF16 = mybir.dt.bfloat16
I32 = mybir.dt.int32
U32 = mybir.dt.uint32
U16 = mybir.dt.uint16
U8 = mybir.dt.uint8
FP8X4 = mybir.dt.float8_e4m3fn_x4
FP4X4 = mybir.dt.float4_e2m1fn_x4
ALU = mybir.AluOpType
ACT = mybir.ActivationFunctionType
AXIS_X = mybir.AxisListType.X

P = 128
PACK = 4
HALF = SLOTS // 2
HALF_PAGES = PAGES // 2
LIST_COLS = SLOTS // 16
LN_FLOOR = 2.0 ** -60
STORE_WIDTHS = (384, 384, 384, 384, 384, 128)


def load_scale_rows(nc, tile, scales):
    for row in range(4):
        nc.sync.dma_start(out=tile[row:P:32, :].bitcast(I32), in_=scales[0, row:16:4, :].bitcast(I32))


def by_page(ap):
    return ap.rearrange("p (g j) -> p g j", j=PAGE)


def over_page(ap):
    return ap.unsqueeze(2).to_broadcast([P, ap.shape[1], PAGE])


def tile_attend_bsharedthreshold_s_kernel(
    tc, query, keys_words, keys_scales, margin, reserve, gout, vals_words, vals_scales, old, offs, out
):
    nc = tc.nc
    with ExitStack() as ctx:
        sb = ctx.enter_context(tc.tile_pool(name="sb", bufs=1))
        psum = ctx.enter_context(tc.psum_pool(name="psum", bufs=1))

        offsets = sb.tile([P, LIST_COLS], U16, name="offsets")
        key_pool = sb.tile([P, T], U16, name="key_pool")
        key_scale_pool = sb.tile([P, T], U8, name="key_scale_pool", tag="key_buf", align_bytes=64)
        val_pool = sb.tile([P, T], U16, name="val_pool")
        val_scale_pool = sb.tile([P, T], U8, name="val_scale_pool")
        q_raw = sb.tile([P, PACK, Q], F32, name="q_raw", tag="operand_a", align_bytes=64)
        g_raw = sb.tile([P, PACK, Q], F32, name="g_raw")
        margin_col = sb.tile([P, 1], F32, name="margin_col")
        reserve_col = sb.tile([P, 1], F32, name="reserve_col")
        total = sb.tile([P, T], F32, name="total")
        placed = sb.tile([P, T], F32, name="placed")
        zero_col = sb.tile([P, 1], F32, name="zero_col")

        nc.gpsimd.memset(zero_col[:], 0.0)
        nc.vector.memset(key_scale_pool[:].bitcast(I32), 0)
        nc.vector.memset(val_scale_pool[:].bitcast(I32), 0)
        nc.vector.memset(placed[:, 0 : T // 2].bitcast(I32), 0)
        nc.gpsimd.memset(placed[:, T // 2 : T].bitcast(I32), 0)

        nc.sync.dma_start(out=key_pool[:].bitcast(I32), in_=keys_words[0].bitcast(I32))
        nc.sync.dma_start(offsets[:], offs)
        load_scale_rows(nc, key_scale_pool, keys_scales)
        nc.sync.dma_start(out=q_raw[:], in_=query.rearrange("(p j) q -> p j q", j=PACK))
        nc.sync.dma_start(out=g_raw[:], in_=gout.rearrange("(p j) q -> p j q", j=PACK))
        nc.sync.dma_start(out=val_pool[:].bitcast(I32), in_=vals_words[0].bitcast(I32))
        nc.sync.dma_start(out=margin_col[:], in_=margin)
        load_scale_rows(nc, val_scale_pool, vals_scales)
        nc.sync.dma_start(out=reserve_col[:], in_=reserve)
        nc.sync.dma_start(out=total[:], in_=old)

        half_col = sb.tile([P, 1], F32, name="half_col")
        nc.scalar.activation(half_col[:], zero_col[:], ACT.Sigmoid)
        minus_half = sb.tile([P, 1], F32, name="minus_half")
        nc.gpsimd.tensor_scalar(minus_half[:], half_col[:], -1.0, 0.0, ALU.mult, ALU.add)

        q_grouped = sb.tile([P, Q, PACK], BF16, name="q_grouped", align_bytes=64)
        g_grouped = sb.tile([P, Q, PACK], BF16, name="g_grouped", align_bytes=64)
        for grouped, raw in ((q_grouped, q_raw), (g_grouped, g_raw)):
            nc.scalar.copy(
                grouped[:].rearrange("p (c i) j -> p c j i", i=4), raw[:].rearrange("p j (c i) -> p c j i", i=4)
            )

        halves = [slice(h * HALF, (h + 1) * HALF) for h in range(2)]
        page_halves = [slice(h * HALF_PAGES, (h + 1) * HALF_PAGES) for h in range(2)]
        list_halves = [offsets[:, h * LIST_COLS // 2 : (h + 1) * LIST_COLS // 2] for h in range(2)]
        key_words = sb.tile([P, SLOTS], U16, name="key_words", tag="operand_b", align_bytes=64)
        key_bytes = [
            sb.tile([P, HALF], U8, name="key_bytes0", align_bytes=64),
            sb.tile([P, HALF], U8, name="key_bytes1", tag="operand_a", align_bytes=64),
        ]
        q_codes = sb.tile([P, Q], U32, name="q_codes", align_bytes=64)
        q_scales = sb.tile([P, Q], U8, name="q_scales", align_bytes=64)
        nc.vector.tensor_copy(key_words[:], key_pool[:].indirect(offsets[:]))
        nc.vector.tensor_copy(key_bytes[0][:], key_scale_pool[:].indirect(list_halves[0]))
        nc.vector.quantize_mx(
            out=q_codes[:].bitcast(FP8X4), scales=q_scales[:], in_=q_grouped[:].rearrange("p q j -> p (q j)")
        )
        nc.vector.tensor_copy(key_bytes[1][:], key_scale_pool[:].indirect(list_halves[1]))
        scores = [psum.tile([P, HALF], F32, name="scores%d" % h) for h in range(2)]
        for h in range(2):
            nc.tensor.matmul_mx(
                out=scores[h][:],
                lhsT=q_codes[:].bitcast(FP8X4),
                lhsT_scale=q_scales[:],
                rhs=key_words[:, halves[h]].bitcast(FP4X4),
                rhs_scale=key_bytes[h][:],
                start=True,
                stop=True,
            )

        g_codes = sb.tile([P, Q], U32, name="g_codes", tag="key_buf", align_bytes=64)
        g_scales = sb.tile([P, Q], U8, name="g_scales", align_bytes=64)
        nc.vector.quantize_mx(
            out=g_codes[:].bitcast(FP8X4), scales=g_scales[:], in_=g_grouped[:].rearrange("p q j -> p (q j)")
        )

        page_sums = sb.tile([P, PAGES], F32, name="page_sums")
        below = sb.tile([P, SLOTS], F32, name="below")
        sig_neg = sb.tile([P, SLOTS], F32, name="sig_neg")
        for h in range(2):
            nc.vector.tensor_reduce(page_sums[:, page_halves[h]], by_page(scores[h][:]), AXIS_X, ALU.add)
        for h in range(2):
            nc.vector.scalar_tensor_tensor(
                by_page(below[:, halves[h]]),
                over_page(page_sums[:, page_halves[h]]),
                1.0 / PAGE,
                by_page(scores[h][:]),
                ALU.mult,
                ALU.subtract,
            )
            nc.scalar.activation(sig_neg[:, halves[h]], below[:, halves[h]], ACT.Sigmoid, bias=margin_col[:])

        val_words = sb.tile([P, SLOTS], U16, name="val_words", tag="operand_b", align_bytes=64)
        nc.vector.tensor_copy(val_words[:], val_pool[:].indirect(offsets[:]))
        val_bytes = sb.tile([P, SLOTS], U8, name="val_bytes", tag="operand_a", align_bytes=64)
        c0 = psum.tile([P, SLOTS], F32, name="c0")
        for h in range(2):
            nc.vector.tensor_copy(val_bytes[:, halves[h]], val_scale_pool[:].indirect(list_halves[h]))
            nc.tensor.matmul_mx(
                out=c0[:, halves[h]],
                lhsT=g_codes[:].bitcast(FP8X4),
                lhsT_scale=g_scales[:],
                rhs=val_words[:, halves[h]].bitcast(FP4X4),
                rhs_scale=val_bytes[:, halves[h]],
                start=True,
                stop=True,
            )

        def inner(tile):
            return tile[:].rearrange("p (c w) -> p c w", c=4)[:, 1:3, :]

        def outer(tile):
            return tile[:].rearrange("p (c w) -> p c w", c=4)[:, 0:4:3, :]

        log_sig = sb.tile([P, SLOTS], F32, name="log_sig")
        neg_p = sb.tile([P, SLOTS], F32, name="neg_p")
        squares = sb.tile([P, SLOTS], F32, name="squares")
        sq_inner = sb.tile([P, 1], F32, name="sq_inner")
        sq_outer = sb.tile([P, 1], F32, name="sq_outer", tag="late_buf")
        for part in (inner, outer):
            nc.scalar.activation(part(log_sig), part(sig_neg), ACT.Ln, bias=LN_FLOOR)
        for part in (inner, outer):
            nc.vector.scalar_tensor_tensor(
                part(neg_p), part(below), margin_col[:], part(log_sig), ALU.add, ALU.min
            )
        partial = sb.tile([P, 1], F32, name="partial")
        norm_sq = sb.tile([P, 1], F32, name="norm_sq")
        nc.scalar.activation(inner(squares), inner(neg_p), ACT.Square, accum_out=sq_inner[:])
        nc.scalar.activation(partial[:], sq_inner[:], ACT.Identity, bias=reserve_col[:])
        nc.scalar.activation(outer(squares), outer(neg_p), ACT.Square, accum_out=sq_outer[:])
        nc.scalar.activation(norm_sq[:], sq_outer[:], ACT.Identity, bias=partial[:])

        products = sb.tile([P, SLOTS], F32, name="products")
        dot_inner = sb.tile([P, 1], F32, name="dot_inner")
        dot_outer = sb.tile([P, 1], F32, name="dot_outer")
        for part, dot in ((inner, dot_inner), (outer, dot_outer)):
            nc.vector.scalar_tensor_tensor(
                part(products), part(c0), -1.0, part(neg_p), ALU.mult, ALU.mult, accum_out=dot[:]
            )
        inv_norm_sq = sb.tile([P, 1], F32, name="inv_norm_sq")
        nc.vector.reciprocal(inv_norm_sq[:], norm_sq[:])
        inv_norm = sb.tile([P, 1], F32, name="inv_norm")
        nc.gpsimd.tensor_tensor(inv_norm[:], norm_sq[:], minus_half[:], ALU.pow)
        sig16 = sb.tile([P, SLOTS], F32, name="sig16", tag="late_buf")
        nc.scalar.activation(sig16[:], sig_neg[:], ACT.Identity, bias=16.0, scale=-16.0)

        pull = sb.tile([P, 1], F32, name="pull")
        nc.vector.tensor_scalar(pull[:], dot_inner[:], dot_outer[:], inv_norm_sq[:], ALU.add, ALU.mult)
        dp_n2 = sb.tile([P, SLOTS], F32, name="dp_n2")
        for h in range(2):
            nc.vector.scalar_tensor_tensor(
                dp_n2[:, halves[h]], neg_p[:, halves[h]], pull[:], c0[:, halves[h]], ALU.mult, ALU.add
            )
        direct = sb.tile([P, SLOTS], F32, name="direct")
        direct_sums = sb.tile([P, PAGES], F32, name="direct_sums")
        shared = sb.tile([P, SLOTS], F32, name="shared")
        for h in range(2):
            nc.vector.scalar_tensor_tensor(
                direct[:, halves[h]], dp_n2[:, halves[h]], inv_norm[:], sig16[:, halves[h]], ALU.mult, ALU.mult
            )
        for h in range(2):
            nc.vector.tensor_reduce(direct_sums[:, page_halves[h]], by_page(direct[:, halves[h]]), AXIS_X, ALU.add)
            nc.scalar.activation(
                by_page(shared[:, halves[h]]), over_page(direct_sums[:, page_halves[h]]), ACT.Copy, scale=-1.0 / PAGE
            )
        for h in range(2):
            nc.vector.tensor_tensor(
                placed[:].indirect(list_halves[h]), direct[:, halves[h]], shared[:, halves[h]], ALU.add
            )

        start = 0
        for n, width in enumerate(STORE_WIDTHS):
            cols = slice(start, start + width)
            nc.vector.tensor_tensor(total[:, cols], total[:, cols], placed[:, cols], ALU.add)
            queue = nc.sync if n % 2 == 0 else nc.scalar
            queue.dma_start(out=out[:, cols], in_=total[:, cols])
            start += width
